import numpy as np
import ml_dtypes


def mxq(x, axis, fmt="e4m3"):
    dtype, down = {"e4m3": (ml_dtypes.float8_e4m3fn, 7), "e5m2": (ml_dtypes.float8_e5m2, 14)}[fmt]
    v = np.moveaxis(np.asarray(x, np.float32).astype(ml_dtypes.bfloat16).astype(np.float64), axis, -1)
    blocks = v.reshape(v.shape[:-1] + (-1, 32))
    amax = np.abs(blocks).max(-1, keepdims=True)
    byte = np.maximum(np.where(amax > 0, np.frexp(amax)[1] - 1 + 127, 0) - down, 1)
    scale = np.exp2(byte - 127.0)
    codes = (blocks / scale).astype(np.float32).astype(dtype).astype(np.float64)
    return np.moveaxis((codes * scale).reshape(v.shape), -1, axis)


WIDE = False


def mx_kscale(k):
    if not WIDE:
        return np.ones(k)
    levels = np.array([30, -30])
    if k % 512:
        return np.exp2(np.random.permutation(np.resize(levels, k // 32))).repeat(32)
    a = np.empty((k // 512, 16))
    for p in range(k // 512):
        a[p, :8] = np.random.permutation(np.resize(levels, 8))
        for g in range(8):
            far = levels[np.abs(levels - a[p, g]) >= 10]
            a[p, g + 8] = far[np.random.randint(len(far))]
    return np.exp2(a.ravel()).repeat(32)


def f64(x):
    return np.asarray(x).astype(np.float64)


def striped(idx):
    return np.tile(np.asarray(idx).reshape(-1, 16).T, (8, 1)).astype(np.uint16)


def unstriped(offs):
    return offs[:16].T.reshape(-1).astype(np.int64)


E2M1 = np.array([0.0, 0.5, 1.0, 1.5, 2.0, 3.0, 4.0, 6.0, -0.0, -0.5, -1.0, -1.5, -2.0, -3.0, -4.0, -6.0])


def pack_weight(w, fmt):
    k, n = w.shape
    w = f64(np.asarray(w, np.float32).astype(ml_dtypes.bfloat16)).reshape(k // 32, 32, n)
    amax = np.abs(w).max(1)
    if fmt in ("e4m3", "e5m2"):
        byte = np.frexp(amax)[1] - 1 + 127 - (7 if fmt == "e4m3" else 14)
    else:
        mant, ex = np.frexp(amax / 6.0)
        byte = np.where(mant > 0.5, ex, ex - 1) + 127
    byte = np.clip(np.where(amax > 0, byte, 1), 1, 254)
    scaled = (w * np.exp2(127.0 - byte)[:, None, :]).reshape(k, n).astype(np.float32)
    by_word = np.ascontiguousarray(scaled.reshape(k // 512, 128, 4, n).transpose(0, 1, 3, 2))
    if fmt in ("e4m3", "e5m2"):
        words = by_word.astype(ml_dtypes.float8_e4m3fn if fmt == "e4m3" else ml_dtypes.float8_e5m2).view(np.uint8)
    else:
        c = by_word.astype(ml_dtypes.float4_e2m1fn).view(np.uint8) & 0xF
        words = (c[..., 0::2] | (c[..., 1::2] << 4)).reshape(k // 512, 128, 2 * n)
    return np.ascontiguousarray(words), np.ascontiguousarray(byte.astype(np.uint8).reshape(k // 512, 16, n))


def unpack_weight(words, scales, fmt):
    g, _, n = scales.shape
    words = np.ascontiguousarray(words).reshape(g, 128, n, -1)
    if fmt in ("e4m3", "e5m2"):
        vals = words.view(ml_dtypes.float8_e4m3fn if fmt == "e4m3" else ml_dtypes.float8_e5m2).astype(np.float64)
    else:
        nib = np.empty((g, 128, n, 4), np.uint8)
        nib[..., 0::2] = words & 0xF
        nib[..., 1::2] = words >> 4
        vals = E2M1[nib]
    vals = vals * np.repeat(np.exp2(scales.astype(np.float64) - 127.0), 8, axis=1)[..., None]
    return vals.transpose(0, 1, 3, 2).reshape(g * 512, n)


def e4m3fn_bytes(y):
    return np.clip(np.asarray(y, np.float64), -448.0, 448.0).astype(np.float32).astype(ml_dtypes.float8_e4m3fn).view(np.uint8)


def e4m3fn_values(b):
    return np.asarray(b, np.uint8).view(ml_dtypes.float8_e4m3fn).astype(np.float64)


K, T, J, R, V, D, I, N, E = 512, 1024, 256, 512, 1024, 2048, 1024, 256, 512


def setup_inputs():
    n = np.random.standard_normal
    idx = np.random.permutation(V)[:R]
    idx2 = np.random.permutation(T)[:J]
    idx3 = np.random.permutation(D)[:I]
    idx4 = np.random.permutation(E)[:J]
    fk = mx_kscale(K)
    fr = mx_kscale(R)
    xtp = pack_weight(n((K, T)) / fk[:, None], "e2m1")
    wtp = pack_weight(n((K, V)) * 1 / np.sqrt(K) * fk[:, None], "e5m2")
    wbp = pack_weight(n((R, N)) * 1 / np.sqrt(R) / fr[:, None], "e4m3")
    return {
        "xt_words": xtp[0],
        "xt_scales": xtp[1],
        "wt_words": wtp[0],
        "wt_scales": wtp[1],
        "ca": e4m3fn_bytes(60.0 * n((R, D))),
        "st": (np.random.uniform(0.004, 0.012, (R, 1)) * fr[:, None]).astype(np.float32),
        "wb_words": wbp[0],
        "wb_scales": wbp[1],
        "so": (np.random.uniform(0.5, 1.6, (N, 1))).astype(np.float32),
        "offs": striped(idx),
        "offs2": striped(idx2),
        "offs3": striped(idx3),
        "offs4": striped(idx4),
    }


def reference(xt_words, xt_scales, wt_words, wt_scales, ca, st, wb_words, wb_scales, so, offs, offs2, offs3, offs4):
    idx = unstriped(offs)
    idx2 = unstriped(offs2)
    idx3 = unstriped(offs3)
    idx4 = unstriped(offs4)
    xtu = unpack_weight(xt_words, xt_scales, "e2m1")
    wtu = unpack_weight(wt_words, wt_scales, "e5m2")
    wbu = unpack_weight(wb_words, wb_scales, "e4m3")
    wtidxg = wtu[:, idx]
    xtidx2g = xtu[:, idx2]
    a = wtidxg.T @ xtidx2g
    m1 = e4m3fn_values(ca)[:, idx3].reshape(R, J, I // J).max(axis=2)
    g1 = m1 * f64(st)
    hid = a * g1
    hidq = mxq(hid, 0, "e4m3")
    p = wbu.T @ hidq
    y = np.zeros((N, E))
    y[:, idx4] = p * f64(so)
    return y

@@ -1,0 +1,169 @@
+from contextlib import ExitStack
+
+import concourse.mybir as mybir
+
+K, T, J, R, V, D, I, N, E = 512, 1024, 256, 512, 1024, 2048, 1024, 256, 512
+FLOPS = 2 * K * R * J + 2 * R * N * J
+
+F32 = mybir.dt.float32
+BF16 = mybir.dt.bfloat16
+I32 = mybir.dt.int32
+U32 = mybir.dt.uint32
+U16 = mybir.dt.uint16
+U8 = mybir.dt.uint8
+FP8 = mybir.dt.float8_e4m3fn
+E4M3X4 = mybir.dt.float8_e4m3fn_x4
+E5M2X4 = mybir.dt.float8_e5m2_x4
+E2M1X4 = mybir.dt.float4_e2m1fn_x4
+COPY = mybir.ActivationFunctionType.Copy
+MAX = mybir.AluOpType.max
+MULT = mybir.AluOpType.mult
+
+P = 128
+PACK = 4
+POOL = I // J
+HALF = 128
+CHUNKS = [(0, 128), (128, 192), (192, 256)]
+
+
+def tile_list_pooledentries_kernel(tc, xt_words, xt_scales, wt_words, wt_scales, ca, st, wb_words, wb_scales, so, offs, offs2, offs3, offs4, out):
+    nc = tc.nc
+    with ExitStack() as ctx:
+        lists = ctx.enter_context(tc.tile_pool(name="lists", bufs=1))
+        sb = ctx.enter_context(tc.tile_pool(name="sb", bufs=1))
+        ps = ctx.enter_context(tc.psum_pool(name="ps", bufs=1))
+
+        def tile(shape, dtype, name, tag=None):
+            return sb.tile(shape, dtype, name=name, tag=tag or name, align_bytes=64)
+
+        l_wt = lists.tile([P, R // 16], U16, name="l_wt")
+        l_xt = lists.tile([P, J // 16], U16, name="l_xt")
+        l_ca = lists.tile([P, I // 16], U16, name="l_ca")
+        l_out = lists.tile([P, J // 16], U16, name="l_out")
+
+        wt_s = tile([P, V], U8, "wt_s")
+        xt_s = tile([P, T], U8, "xt_s")
+        wb_s = tile([P, N], U8, "wb_s")
+        for plane in (wt_s, xt_s, wb_s):
+            nc.vector.memset(plane[:].bitcast(I32), 0)
+        pages = [tile([P, E], F32, "page%d" % h) for h in range(2)]
+        for page in pages:
+            nc.vector.memset(page[:], 0.0)
+
+        def load_scales(plane, src):
+            for q in range(4):
+                nc.sync.dma_start(plane[32 * q : 32 * q + 4, :].bitcast(I32), src[0, 4 * q : 4 * q + 4, :].bitcast(I32))
+
+        ca_rows = ca.rearrange("(p t) d -> t p d", t=PACK)
+        ca_t = [tile([P, D], U8, "ca%d" % t) for t in range(PACK)]
+        nc.sync.dma_start(l_ca[:], offs3)
+        for t in range(PACK):
+            nc.sync.dma_start(ca_t[t][:], ca_rows[t])
+        wt_w = tile([P, V], U32, "wt_w")
+        xt_w = tile([P, T], U16, "xt_w")
+        wb_w = tile([P, N], U32, "wb_w")
+        nc.sync.dma_start(l_wt[:], offs)
+        nc.sync.dma_start(wt_w[:].bitcast(I32), wt_words[0].rearrange("p c r -> p (c r)").bitcast(I32))
+        nc.sync.dma_start(l_xt[:], offs2)
+        nc.sync.dma_start(xt_w[:].bitcast(I32), xt_words[0].bitcast(I32))
+        load_scales(wt_s, wt_scales)
+        load_scales(xt_s, xt_scales)
+        st_sb = tile([P, PACK], F32, "st_sb")
+        nc.sync.dma_start(st_sb[:], st.rearrange("(p t) o -> p (t o)", t=PACK))
+        nc.sync.dma_start(wb_w[:].bitcast(I32), wb_words[0].rearrange("p c r -> p (c r)").bitcast(I32))
+        load_scales(wb_s, wb_scales)
+        so_sb = [tile([P, 1], F32, "so%d" % h) for h in range(2)]
+        for h in range(2):
+            nc.sync.dma_start(so_sb[h][:], so[h * P : (h + 1) * P, :])
+        nc.sync.dma_start(l_out[:], offs4)
+
+        vals = {}
+
+        def look_up(c):
+            j0, j1 = CHUNKS[c]
+            n = (j1 - j0) * POOL
+            vals[c] = tile([P, PACK, n], F32, "vals%d" % c)
+            picked = tile([P, PACK, n], U8, "picked%d" % c, tag={1: "xt_s", 2: "hid0"}.get(c))
+            for t in range(PACK):
+                nc.vector.tensor_copy(picked[:, t, :], ca_t[t][:].indirect(l_ca[:, j0 * POOL // 16 : j1 * POOL // 16]))
+                nc.scalar.activation(vals[c][:, t, :], picked[:, t, :].bitcast(FP8), COPY)
+
+        scaled = {}
+
+        def first_product():
+            g_wt_w = tile([P, PACK, P], U32, "g_wt_w")
+            g_wt_s = tile([P, PACK, P], U8, "g_wt_s")
+            g_xt_w = tile([P, J], U16, "g_xt_w")
+            g_xt_s = tile([P, J], U8, "g_xt_s")
+            nc.vector.tensor_copy(g_wt_w[:].rearrange("p t m -> p m t"), wt_w[:].indirect(l_wt[:]))
+            nc.vector.tensor_copy(g_xt_w[:], xt_w[:].indirect(l_xt[:]))
+            nc.vector.tensor_copy(g_wt_s[:].rearrange("p t m -> p m t"), wt_s[:].indirect(l_wt[:]))
+            nc.vector.tensor_copy(g_xt_s[:], xt_s[:].indirect(l_xt[:]))
+            for u in range(J // HALF):
+                cols = slice(u * HALF, (u + 1) * HALF)
+                acc = ps.tile([P, PACK, HALF], F32, name="acc%d" % u)
+                by_t = tile([P, PACK, HALF], F32, "by_t%d" % u)
+                scaled[u] = tile([P, HALF, PACK], F32, "scaled%d" % u)
+                for t in range(PACK):
+                    nc.tensor.matmul_mx(
+                        out=acc[:, t, :],
+                        lhsT=g_wt_w[:, t, :].bitcast(E5M2X4),
+                        lhsT_scale=g_wt_s[:, t, :],
+                        rhs=g_xt_w[:, cols].bitcast(E2M1X4),
+                        rhs_scale=g_xt_s[:, cols],
+                        start=True,
+                        stop=True,
+                    )
+                for t in range(PACK):
+                    nc.scalar.activation(by_t[:, t, :], acc[:, t, :], COPY, scale=st_sb[:, t : t + 1])
+                nc.scalar.copy(scaled[u][:], by_t[:].rearrange("p t j -> p j t"))
+
+        tops = {}
+
+        def pool(c):
+            j0, j1 = CHUNKS[c]
+            w = j1 - j0
+            four = vals[c][:].rearrange("p t (j q) -> p j t q", q=POOL)
+            pairs = tile([P, w, PACK, 2], F32, "pairs%d" % c)
+            nc.vector.tensor_tensor(pairs[:], four[:, :, :, 0:2], four[:, :, :, 2:4], MAX)
+            tops[c] = tile([P, w, PACK], F32, "tops%d" % c)
+            nc.vector.tensor_tensor(tops[c][:], pairs[:, :, :, 0], pairs[:, :, :, 1], MAX)
+
+        def second_product(c):
+            j0, j1 = CHUNKS[c]
+            w = j1 - j0
+            u, a0 = divmod(j0, HALF)
+            hid = tile([P, w, PACK], BF16, "hid%d" % c)
+            nc.vector.tensor_tensor(hid[:], tops[c][:], scaled[u][:, a0 : a0 + w, :], MULT)
+            codes = tile([P, w], U32, "codes%d" % c)
+            plane = tile([P, w], U8, "plane%d" % c)
+            nc.vector.quantize_mx(out=codes[:].bitcast(E4M3X4), scales=plane[:], in_=hid[:].rearrange("p j t -> p (j t)"))
+            prod = ps.tile([P, 2, w], F32, name="prod%d" % c)
+            rows = tile([P, 2, w], F32, "rows%d" % c)
+            for h in range(2):
+                ncols = slice(h * P, (h + 1) * P)
+                nc.tensor.matmul_mx(
+                    out=prod[:, h, :],
+                    lhsT=wb_w[:, ncols].bitcast(E4M3X4),
+                    lhsT_scale=wb_s[:, ncols],
+                    rhs=codes[:].bitcast(E4M3X4),
+                    rhs_scale=plane[:],
+                    start=True,
+                    stop=True,
+                )
+            nc.scalar.copy(rows[:], prod[:])
+            for h in range(2):
+                nc.scalar.activation(pages[h][:].indirect(l_out[:, j0 // 16 : j1 // 16]), rows[:, h, :], COPY, scale=so_sb[h][:])
+
+        look_up(0)
+        first_product()
+        pool(0)
+        look_up(1)
+        second_product(0)
+        look_up(2)
+        pool(1)
+        second_product(1)
+        pool(2)
+        second_product(2)
+        for h in range(2):
+            nc.sync.dma_start(out[h * P : (h + 1) * P, :], pages[h][:])

@@ -16,14 +16,21 @@ E4M3X4 = mybir.dt.float8_e4m3fn_x4
 E5M2X4 = mybir.dt.float8_e5m2_x4
 E2M1X4 = mybir.dt.float4_e2m1fn_x4
 COPY = mybir.ActivationFunctionType.Copy
+RELU = mybir.ActivationFunctionType.Relu
 MAX = mybir.AluOpType.max
 MULT = mybir.AluOpType.mult
+ADD = mybir.AluOpType.add
+SUB = mybir.AluOpType.subtract
 
 P = 128
 PACK = 4
 POOL = I // J
-HALF = 128
+PER_COLUMN = 16
 CHUNKS = [(0, 128), (128, 192), (192, 256)]
+FIRST, MIDDLE, LAST = range(3)
+LONG = 128
+SHORT = 64
+PIECE = SHORT // 2
 
 
 def tile_list_pooledentries_kernel(tc, xt_words, xt_scales, wt_words, wt_scales, ca, st, wb_words, wb_scales, so, offs, offs2, offs3, offs4, out):
@@ -33,137 +40,265 @@ def tile_list_pooledentries_kernel(tc, xt_words, xt_scales, wt_words, wt_scales,
         sb = ctx.enter_context(tc.tile_pool(name="sb", bufs=1))
         ps = ctx.enter_context(tc.psum_pool(name="ps", bufs=1))
 
-        def tile(shape, dtype, name, tag=None):
-            return sb.tile(shape, dtype, name=name, tag=tag or name, align_bytes=64)
+        def tile(shape, dtype, name, in_place_of=None):
+            return sb.tile(shape, dtype, name=name, tag=in_place_of or name, align_bytes=64)
 
-        l_wt = lists.tile([P, R // 16], U16, name="l_wt")
-        l_xt = lists.tile([P, J // 16], U16, name="l_xt")
-        l_ca = lists.tile([P, I // 16], U16, name="l_ca")
-        l_out = lists.tile([P, J // 16], U16, name="l_out")
+        wt_list = lists.tile([P, R // PER_COLUMN], U16, name="wt_list")
+        xt_list = lists.tile([P, J // PER_COLUMN], U16, name="xt_list")
+        ca_list = lists.tile([P, I // PER_COLUMN], U16, name="ca_list")
+        out_list = lists.tile([P, J // PER_COLUMN], U16, name="out_list")
 
         wt_s = tile([P, V], U8, "wt_s")
         xt_s = tile([P, T], U8, "xt_s")
         wb_s = tile([P, N], U8, "wb_s")
-        for plane in (wt_s, xt_s, wb_s):
-            nc.vector.memset(plane[:].bitcast(I32), 0)
+        for scale_tile in (wt_s, xt_s, wb_s):
+            nc.vector.memset(scale_tile[:].bitcast(I32), 0)
         pages = [tile([P, E], F32, "page%d" % h) for h in range(2)]
         for page in pages:
             nc.vector.memset(page[:], 0.0)
 
-        def load_scales(plane, src):
+        def load_scales(scale_tile, src):
             for q in range(4):
-                nc.sync.dma_start(plane[32 * q : 32 * q + 4, :].bitcast(I32), src[0, 4 * q : 4 * q + 4, :].bitcast(I32))
+                nc.sync.dma_start(scale_tile[32 * q : 32 * q + 4, :].bitcast(I32), src[0, 4 * q : 4 * q + 4, :].bitcast(I32))
 
         ca_rows = ca.rearrange("(p t) d -> t p d", t=PACK)
-        ca_t = [tile([P, D], U8, "ca%d" % t) for t in range(PACK)]
-        nc.sync.dma_start(l_ca[:], offs3)
-        for t in range(PACK):
-            nc.sync.dma_start(ca_t[t][:], ca_rows[t])
+        ca_sb = [tile([P, D], U8, "ca%d" % t) for t in range(PACK)]
         wt_w = tile([P, V], U32, "wt_w")
         xt_w = tile([P, T], U16, "xt_w")
         wb_w = tile([P, N], U32, "wb_w")
-        nc.sync.dma_start(l_wt[:], offs)
+        st_sb = tile([P, PACK], F32, "st_sb")
+        so_sb = [tile([P, 1], F32, "so%d" % h) for h in range(2)]
+        nc.sync.dma_start(ca_sb[0][:], ca_rows[0])
+        nc.sync.dma_start(ca_list[:], offs3)
+        nc.sync.dma_start(ca_sb[1][:], ca_rows[1])
+        nc.sync.dma_start(wt_list[:], offs)
         nc.sync.dma_start(wt_w[:].bitcast(I32), wt_words[0].rearrange("p c r -> p (c r)").bitcast(I32))
-        nc.sync.dma_start(l_xt[:], offs2)
+        nc.sync.dma_start(xt_list[:], offs2)
         nc.sync.dma_start(xt_w[:].bitcast(I32), xt_words[0].bitcast(I32))
         load_scales(wt_s, wt_scales)
         load_scales(xt_s, xt_scales)
-        st_sb = tile([P, PACK], F32, "st_sb")
+        nc.sync.dma_start(ca_sb[2][:], ca_rows[2])
+        nc.sync.dma_start(ca_sb[3][:], ca_rows[3])
         nc.sync.dma_start(st_sb[:], st.rearrange("(p t) o -> p (t o)", t=PACK))
         nc.sync.dma_start(wb_w[:].bitcast(I32), wb_words[0].rearrange("p c r -> p (c r)").bitcast(I32))
         load_scales(wb_s, wb_scales)
-        so_sb = [tile([P, 1], F32, "so%d" % h) for h in range(2)]
         for h in range(2):
             nc.sync.dma_start(so_sb[h][:], so[h * P : (h + 1) * P, :])
-        nc.sync.dma_start(l_out[:], offs4)
+        nc.sync.dma_start(out_list[:], offs4)
 
-        vals = {}
+        short_values = {c: tile([P, PACK, SHORT * POOL], F32, "values%d" % c) for c in (MIDDLE, LAST)}
+        early_values = [tile([P, LONG * POOL], F32, "early_values%d" % t) for t in range(2)]
+        late_values = tile([P, 2, LONG * POOL], F32, "late_values")
+        values = {(c, t): short_values[c][:, t, :] for c in (MIDDLE, LAST) for t in range(PACK)}
+        for t in range(2):
+            values[FIRST, t] = early_values[t][:]
+            values[FIRST, 2 + t] = late_values[:, t, :]
+        picked = {}
 
-        def look_up(c):
+        def room_for_bytes(keys, in_place_of=None):
+            j0, j1 = CHUNKS[keys[0][0]]
+            held = tile([P, len(keys), (j1 - j0) * POOL], U8, "picked%d_%d" % keys[0], in_place_of)
+            for i, key in enumerate(keys):
+                picked[key] = held[:, i, :]
+
+        def look_up(c, t):
             j0, j1 = CHUNKS[c]
-            n = (j1 - j0) * POOL
-            vals[c] = tile([P, PACK, n], F32, "vals%d" % c)
-            picked = tile([P, PACK, n], U8, "picked%d" % c, tag={1: "xt_s", 2: "hid0"}.get(c))
-            for t in range(PACK):
-                nc.vector.tensor_copy(picked[:, t, :], ca_t[t][:].indirect(l_ca[:, j0 * POOL // 16 : j1 * POOL // 16]))
-                nc.scalar.activation(vals[c][:, t, :], picked[:, t, :].bitcast(FP8), COPY)
+            entries = ca_list[:, j0 * POOL // PER_COLUMN : j1 * POOL // PER_COLUMN]
+            nc.vector.tensor_copy(picked[c, t], ca_sb[t][:].indirect(entries))
 
-        scaled = {}
+        def widen(c, t):
+            nc.scalar.activation(values[c, t], picked[c, t].bitcast(FP8), COPY)
+
+        got_wt_w = tile([P, PACK, P], U32, "got_wt_w")
+        got_wt_s = tile([P, PACK, P], U8, "got_wt_s")
+        got_xt_w = tile([P, J], U16, "got_xt_w")
+        got_xt_s = tile([P, J], U8, "got_xt_s")
+        stepped = tile([P, PACK, J], F32, "stepped")
+        sums, woven = {}, {}
 
         def first_product():
-            g_wt_w = tile([P, PACK, P], U32, "g_wt_w")
-            g_wt_s = tile([P, PACK, P], U8, "g_wt_s")
-            g_xt_w = tile([P, J], U16, "g_xt_w")
-            g_xt_s = tile([P, J], U8, "g_xt_s")
-            nc.vector.tensor_copy(g_wt_w[:].rearrange("p t m -> p m t"), wt_w[:].indirect(l_wt[:]))
-            nc.vector.tensor_copy(g_xt_w[:], xt_w[:].indirect(l_xt[:]))
-            nc.vector.tensor_copy(g_wt_s[:].rearrange("p t m -> p m t"), wt_s[:].indirect(l_wt[:]))
-            nc.vector.tensor_copy(g_xt_s[:], xt_s[:].indirect(l_xt[:]))
-            for u in range(J // HALF):
-                cols = slice(u * HALF, (u + 1) * HALF)
-                acc = ps.tile([P, PACK, HALF], F32, name="acc%d" % u)
-                by_t = tile([P, PACK, HALF], F32, "by_t%d" % u)
-                scaled[u] = tile([P, HALF, PACK], F32, "scaled%d" % u)
-                for t in range(PACK):
-                    nc.tensor.matmul_mx(
-                        out=acc[:, t, :],
-                        lhsT=g_wt_w[:, t, :].bitcast(E5M2X4),
-                        lhsT_scale=g_wt_s[:, t, :],
-                        rhs=g_xt_w[:, cols].bitcast(E2M1X4),
-                        rhs_scale=g_xt_s[:, cols],
-                        start=True,
-                        stop=True,
-                    )
-                for t in range(PACK):
-                    nc.scalar.activation(by_t[:, t, :], acc[:, t, :], COPY, scale=st_sb[:, t : t + 1])
-                nc.scalar.copy(scaled[u][:], by_t[:].rearrange("p t j -> p j t"))
-
-        tops = {}
-
-        def pool(c):
-            j0, j1 = CHUNKS[c]
-            w = j1 - j0
-            four = vals[c][:].rearrange("p t (j q) -> p j t q", q=POOL)
-            pairs = tile([P, w, PACK, 2], F32, "pairs%d" % c)
-            nc.vector.tensor_tensor(pairs[:], four[:, :, :, 0:2], four[:, :, :, 2:4], MAX)
-            tops[c] = tile([P, w, PACK], F32, "tops%d" % c)
-            nc.vector.tensor_tensor(tops[c][:], pairs[:, :, :, 0], pairs[:, :, :, 1], MAX)
-
-        def second_product(c):
-            j0, j1 = CHUNKS[c]
-            w = j1 - j0
-            u, a0 = divmod(j0, HALF)
-            hid = tile([P, w, PACK], BF16, "hid%d" % c)
-            nc.vector.tensor_tensor(hid[:], tops[c][:], scaled[u][:, a0 : a0 + w, :], MULT)
-            codes = tile([P, w], U32, "codes%d" % c)
-            plane = tile([P, w], U8, "plane%d" % c)
-            nc.vector.quantize_mx(out=codes[:].bitcast(E4M3X4), scales=plane[:], in_=hid[:].rearrange("p j t -> p (j t)"))
-            prod = ps.tile([P, 2, w], F32, name="prod%d" % c)
-            rows = tile([P, 2, w], F32, "rows%d" % c)
-            for h in range(2):
-                ncols = slice(h * P, (h + 1) * P)
+            nc.vector.tensor_copy(got_wt_w[:].rearrange("p t m -> p m t"), wt_w[:].indirect(wt_list[:]))
+            nc.vector.tensor_copy(got_xt_w[:], xt_w[:].indirect(xt_list[:]))
+            nc.vector.tensor_copy(got_wt_s[:].rearrange("p t m -> p m t"), wt_s[:].indirect(wt_list[:]))
+            nc.vector.tensor_copy(got_xt_s[:], xt_s[:].indirect(xt_list[:]))
+            for t in range(PACK):
+                if t % 2 == 0:
+                    bank = ps.tile([P, 2, J], F32, name="sums%d" % (t // 2))
+                sums[t] = bank[:, t % 2, :]
                 nc.tensor.matmul_mx(
-                    out=prod[:, h, :],
-                    lhsT=wb_w[:, ncols].bitcast(E4M3X4),
-                    lhsT_scale=wb_s[:, ncols],
-                    rhs=codes[:].bitcast(E4M3X4),
-                    rhs_scale=plane[:],
+                    out=sums[t],
+                    lhsT=got_wt_w[:, t, :].bitcast(E5M2X4),
+                    lhsT_scale=got_wt_s[:, t, :],
+                    rhs=got_xt_w[:].bitcast(E2M1X4),
+                    rhs_scale=got_xt_s[:],
                     start=True,
                     stop=True,
                 )
-            nc.scalar.copy(rows[:], prod[:])
-            for h in range(2):
-                nc.scalar.activation(pages[h][:].indirect(l_out[:, j0 // 16 : j1 // 16]), rows[:, h, :], COPY, scale=so_sb[h][:])
 
-        look_up(0)
+        def apply_step(t):
+            nc.scalar.activation(stepped[:, t, :], sums[t], COPY, scale=st_sb[:, t : t + 1])
+
+        def weave(u):
+            woven[u] = tile([P, LONG, PACK], F32, "woven%d" % u)
+            nc.scalar.copy(woven[u][:], stepped[:, :, u * LONG : (u + 1) * LONG].rearrange("p t j -> p j t"))
+
+        hid = {}
+
+        def larger_off_vector(dst, x, y, name):
+            diff = tile([P, LONG, 2], F32, name + "_diff")
+            rise = tile([P, LONG, 2], F32, name + "_rise")
+            nc.gpsimd.tensor_tensor(diff[:], x, y, SUB)
+            nc.scalar.activation(rise[:], diff[:], RELU)
+            nc.gpsimd.tensor_tensor(dst, rise[:], y, ADD)
+
+        early_pairs = tile([P, 2, LONG, 2], F32, "early_pairs")
+        first_tops = tile([P, 2, LONG, 2], F32, "first_tops")
+        late_pairs = tile([P, LONG, 2, 2], F32, "late_pairs")
+
+        def early_maxima():
+            for t in range(2):
+                four = early_values[t][:].rearrange("p (j q) -> p j q", q=POOL)
+                larger_off_vector(early_pairs[:, t], four[:, :, 0:2], four[:, :, 2:4], "early%d" % t)
+            two = early_pairs[:].rearrange("p t j e -> p j t e")
+            larger_off_vector(first_tops[:, 0], two[:, :, :, 0], two[:, :, :, 1], "early_top")
+
+        def late_round_one():
+            four = late_values[:].rearrange("p t (j q) -> p j t q", q=POOL)
+            nc.vector.tensor_tensor(late_pairs[:], four[:, :, :, 0:2], four[:, :, :, 2:4], MAX)
+
+        def late_round_two():
+            nc.vector.tensor_tensor(first_tops[:, 1], late_pairs[:, :, :, 0], late_pairs[:, :, :, 1], MAX)
+
+        def first_hid():
+            hid[FIRST] = tile([P, LONG, PACK], BF16, "first_hid")
+            nc.gpsimd.tensor_tensor(
+                hid[FIRST][:].rearrange("p j (a b) -> p j a b", b=2),
+                first_tops[:].rearrange("p a j b -> p j a b"),
+                woven[0][:].rearrange("p j (a b) -> p j a b", b=2),
+                MULT,
+            )
+
+        pairs, tops = {}, {}
+
+        def round_one(key, c, slots, groups):
+            four = short_values[c][:].rearrange("p t (j q) -> p j t q", q=POOL)[:, slots, groups]
+            nc.vector.tensor_tensor(pairs[key][:, :, groups, :], four[:, :, :, 0:2], four[:, :, :, 2:4], MAX)
+
+        def round_two(key, width):
+            tops[key] = tile([P, width, PACK], F32, "tops_" + key)
+            nc.vector.tensor_tensor(tops[key][:], pairs[key][:, :, :, 0], pairs[key][:, :, :, 1], MAX)
+
+        def make_hid(key, c, slots):
+            first = CHUNKS[c][0] - LONG
+            factors = woven[1][:, first + slots.start : first + slots.stop, :]
+            nc.vector.tensor_tensor(hid[c][:, slots, :], tops[key][:], factors, MULT)
+
+        products, banks, rows = {}, {}, {}
+
+        def second_product(c):
+            width = CHUNKS[c][1] - CHUNKS[c][0]
+            codes = tile([P, width], U32, "codes%d" % c)
+            scales = tile([P, width], U8, "scales%d" % c)
+            nc.vector.quantize_mx(out=codes[:].bitcast(E4M3X4), scales=scales[:], in_=hid[c][:].rearrange("p j t -> p (j t)"))
+            if c == LAST:
+                for h in range(2):
+                    products[c, h] = ps.tile([P, width], F32, name="product%d_%d" % (c, h))[:]
+            else:
+                banks[c] = ps.tile([P, 2, width], F32, name="product%d" % c)
+                for h in range(2):
+                    products[c, h] = banks[c][:, h, :]
+            for h in range(2):
+                nc.tensor.matmul_mx(
+                    out=products[c, h],
+                    lhsT=wb_w[:, h * P : (h + 1) * P].bitcast(E4M3X4),
+                    lhsT_scale=wb_s[:, h * P : (h + 1) * P],
+                    rhs=codes[:].bitcast(E4M3X4),
+                    rhs_scale=scales[:],
+                    start=True,
+                    stop=True,
+                )
+
+        def to_sbuf(c, h, copy, in_place_of=None):
+            rows[c, h] = tile([P, CHUNKS[c][1] - CHUNKS[c][0]], F32, "rows%d_%d" % (c, h), in_place_of)[:]
+            copy(rows[c, h], products[c, h])
+
+        def put(c, h):
+            j0, j1 = CHUNKS[c]
+            columns = out_list[:, j0 // PER_COLUMN : j1 // PER_COLUMN]
+            nc.scalar.activation(pages[h][:].indirect(columns), rows[c, h], COPY, scale=so_sb[h][:])
+
+        for t in range(PACK):
+            room_for_bytes([(FIRST, t)])
+        for t in range(2):
+            look_up(FIRST, t)
+            widen(FIRST, t)
+        early_maxima()
         first_product()
-        pool(0)
-        look_up(1)
-        second_product(0)
-        look_up(2)
-        pool(1)
-        second_product(1)
-        pool(2)
-        second_product(2)
+        look_up(FIRST, 2)
+        widen(FIRST, 2)
+        apply_step(0)
+        look_up(FIRST, 3)
+        widen(FIRST, 3)
+        for t in range(1, PACK):
+            apply_step(t)
+        weave(0)
+
+        room_for_bytes([(MIDDLE, 0)], "picked0_2")
+        look_up(MIDDLE, 0)
+        late_round_one()
+        room_for_bytes([(MIDDLE, 1)], "picked0_3")
+        look_up(MIDDLE, 1)
+        late_round_two()
+        first_hid()
+        beside_first_hid = [(MIDDLE, 2), (MIDDLE, 3), (LAST, 0), (LAST, 1)]
+        room_for_bytes(beside_first_hid, "late_values")
+        for c, t in beside_first_hid:
+            look_up(c, t)
+        for t in range(PACK):
+            widen(MIDDLE, t)
+        weave(1)
+        for t in range(2):
+            widen(LAST, t)
+        second_product(FIRST)
+        to_sbuf(FIRST, 0, nc.scalar.copy)
+        put(FIRST, 0)
+
+        everything = slice(0, PACK)
+        whole = slice(0, SHORT)
+        pairs["middle"] = tile([P, SHORT, PACK, 2], F32, "pairs_middle", "first_tops")
+        round_one("middle", MIDDLE, whole, everything)
+        room_for_bytes([(LAST, 2), (LAST, 3)], "woven0")
+        for t in (2, 3):
+            look_up(LAST, t)
+            widen(LAST, t)
+        round_two("middle", SHORT)
+        to_sbuf(FIRST, 1, nc.scalar.copy, "ca3")
+        put(FIRST, 1)
+
+        pieces = [("piece%d" % i, slice(i * PIECE, (i + 1) * PIECE)) for i in range(2)]
+        for key, slots in pieces:
+            pairs[key] = tile([P, PIECE, PACK, 2], F32, "pairs_" + key)
+            round_one(key, LAST, slots, slice(0, 2))
+        hid[MIDDLE] = tile([P, SHORT, PACK], BF16, "middle_hid")
+        make_hid("middle", MIDDLE, whole)
+        for key, slots in pieces:
+            round_one(key, LAST, slots, slice(2, PACK))
+        second_product(MIDDLE)
+        for key, slots in pieces:
+            round_two(key, PIECE)
+        middle_rows = tile([P, 2, SHORT], F32, "middle_rows")
+        nc.vector.tensor_copy(middle_rows[:], banks[MIDDLE][:])
         for h in range(2):
-            nc.sync.dma_start(out[h * P : (h + 1) * P, :], pages[h][:])
+            rows[MIDDLE, h] = middle_rows[:, h, :]
+            put(MIDDLE, h)
+        hid[LAST] = tile([P, SHORT, PACK], BF16, "last_hid")
+        for key, slots in pieces:
+            make_hid(key, LAST, slots)
+        second_product(LAST)
+        for h in range(2):
+            to_sbuf(LAST, h, nc.vector.tensor_copy)
+        for h in range(2):
+            put(LAST, h)
+
+        nc.sync.dma_start(out[0:P, :], pages[0][:])
+        nc.scalar.dma_start(out[P : 2 * P, :], pages[1][:])

from contextlib import ExitStack

import concourse.mybir as mybir

K, T, J, R, V, D, I, N, E = 512, 1024, 256, 512, 1024, 2048, 1024, 256, 512
FLOPS = 2 * K * R * J + 2 * R * N * J

F32 = mybir.dt.float32
BF16 = mybir.dt.bfloat16
I32 = mybir.dt.int32
U32 = mybir.dt.uint32
U16 = mybir.dt.uint16
U8 = mybir.dt.uint8
FP8 = mybir.dt.float8_e4m3fn
E4M3X4 = mybir.dt.float8_e4m3fn_x4
E5M2X4 = mybir.dt.float8_e5m2_x4
E2M1X4 = mybir.dt.float4_e2m1fn_x4
COPY = mybir.ActivationFunctionType.Copy
RELU = mybir.ActivationFunctionType.Relu
MAX = mybir.AluOpType.max
MULT = mybir.AluOpType.mult
ADD = mybir.AluOpType.add
SUB = mybir.AluOpType.subtract

P = 128
PACK = 4
POOL = I // J
PER_COLUMN = 16
CHUNKS = [(0, 128), (128, 192), (192, 256)]
FIRST, MIDDLE, LAST = range(3)
LONG = 128
SHORT = 64
PIECE = SHORT // 2


def tile_list_pooledentries_kernel(tc, xt_words, xt_scales, wt_words, wt_scales, ca, st, wb_words, wb_scales, so, offs, offs2, offs3, offs4, out):
    nc = tc.nc
    with ExitStack() as ctx:
        lists = ctx.enter_context(tc.tile_pool(name="lists", bufs=1))
        sb = ctx.enter_context(tc.tile_pool(name="sb", bufs=1))
        ps = ctx.enter_context(tc.psum_pool(name="ps", bufs=1))

        def tile(shape, dtype, name, in_place_of=None):
            return sb.tile(shape, dtype, name=name, tag=in_place_of or name, align_bytes=64)

        wt_list = lists.tile([P, R // PER_COLUMN], U16, name="wt_list")
        xt_list = lists.tile([P, J // PER_COLUMN], U16, name="xt_list")
        ca_list = lists.tile([P, I // PER_COLUMN], U16, name="ca_list")
        out_list = lists.tile([P, J // PER_COLUMN], U16, name="out_list")

        wt_s = tile([P, V], U8, "wt_s")
        xt_s = tile([P, T], U8, "xt_s")
        wb_s = tile([P, N], U8, "wb_s")
        for scale_tile in (wt_s, xt_s, wb_s):
            nc.vector.memset(scale_tile[:].bitcast(I32), 0)
        pages = [tile([P, E], F32, "page%d" % h) for h in range(2)]
        for page in pages:
            nc.vector.memset(page[:], 0.0)

        def load_scales(scale_tile, src):
            for q in range(4):
                nc.sync.dma_start(scale_tile[32 * q : 32 * q + 4, :].bitcast(I32), src[0, 4 * q : 4 * q + 4, :].bitcast(I32))

        ca_rows = ca.rearrange("(p t) d -> t p d", t=PACK)
        ca_sb = [tile([P, D], U8, "ca%d" % t) for t in range(PACK)]
        wt_w = tile([P, V], U32, "wt_w")
        xt_w = tile([P, T], U16, "xt_w")
        wb_w = tile([P, N], U32, "wb_w")
        st_sb = tile([P, PACK], F32, "st_sb")
        so_sb = [tile([P, 1], F32, "so%d" % h) for h in range(2)]
        nc.sync.dma_start(ca_sb[0][:], ca_rows[0])
        nc.sync.dma_start(ca_list[:], offs3)
        nc.sync.dma_start(ca_sb[1][:], ca_rows[1])
        nc.sync.dma_start(wt_list[:], offs)
        nc.sync.dma_start(wt_w[:].bitcast(I32), wt_words[0].rearrange("p c r -> p (c r)").bitcast(I32))
        nc.sync.dma_start(xt_list[:], offs2)
        nc.sync.dma_start(xt_w[:].bitcast(I32), xt_words[0].bitcast(I32))
        load_scales(wt_s, wt_scales)
        load_scales(xt_s, xt_scales)
        nc.sync.dma_start(ca_sb[2][:], ca_rows[2])
        nc.sync.dma_start(ca_sb[3][:], ca_rows[3])
        nc.sync.dma_start(st_sb[:], st.rearrange("(p t) o -> p (t o)", t=PACK))
        nc.sync.dma_start(wb_w[:].bitcast(I32), wb_words[0].rearrange("p c r -> p (c r)").bitcast(I32))
        load_scales(wb_s, wb_scales)
        for h in range(2):
            nc.sync.dma_start(so_sb[h][:], so[h * P : (h + 1) * P, :])
        nc.sync.dma_start(out_list[:], offs4)

        short_values = {c: tile([P, PACK, SHORT * POOL], F32, "values%d" % c) for c in (MIDDLE, LAST)}
        early_values = [tile([P, LONG * POOL], F32, "early_values%d" % t) for t in range(2)]
        late_values = tile([P, 2, LONG * POOL], F32, "late_values")
        values = {(c, t): short_values[c][:, t, :] for c in (MIDDLE, LAST) for t in range(PACK)}
        for t in range(2):
            values[FIRST, t] = early_values[t][:]
            values[FIRST, 2 + t] = late_values[:, t, :]
        picked = {}

        def room_for_bytes(keys, in_place_of=None):
            j0, j1 = CHUNKS[keys[0][0]]
            held = tile([P, len(keys), (j1 - j0) * POOL], U8, "picked%d_%d" % keys[0], in_place_of)
            for i, key in enumerate(keys):
                picked[key] = held[:, i, :]

        def look_up(c, t):
            j0, j1 = CHUNKS[c]
            entries = ca_list[:, j0 * POOL // PER_COLUMN : j1 * POOL // PER_COLUMN]
            nc.vector.tensor_copy(picked[c, t], ca_sb[t][:].indirect(entries))

        def widen(c, t):
            nc.scalar.activation(values[c, t], picked[c, t].bitcast(FP8), COPY)

        got_wt_w = tile([P, PACK, P], U32, "got_wt_w")
        got_wt_s = tile([P, PACK, P], U8, "got_wt_s")
        got_xt_w = tile([P, J], U16, "got_xt_w")
        got_xt_s = tile([P, J], U8, "got_xt_s")
        stepped = tile([P, PACK, J], F32, "stepped")
        sums, woven = {}, {}

        def first_product():
            nc.vector.tensor_copy(got_wt_w[:].rearrange("p t m -> p m t"), wt_w[:].indirect(wt_list[:]))
            nc.vector.tensor_copy(got_xt_w[:], xt_w[:].indirect(xt_list[:]))
            nc.vector.tensor_copy(got_wt_s[:].rearrange("p t m -> p m t"), wt_s[:].indirect(wt_list[:]))
            nc.vector.tensor_copy(got_xt_s[:], xt_s[:].indirect(xt_list[:]))
            for t in range(PACK):
                if t % 2 == 0:
                    bank = ps.tile([P, 2, J], F32, name="sums%d" % (t // 2))
                sums[t] = bank[:, t % 2, :]
                nc.tensor.matmul_mx(
                    out=sums[t],
                    lhsT=got_wt_w[:, t, :].bitcast(E5M2X4),
                    lhsT_scale=got_wt_s[:, t, :],
                    rhs=got_xt_w[:].bitcast(E2M1X4),
                    rhs_scale=got_xt_s[:],
                    start=True,
                    stop=True,
                )

        def apply_step(t):
            nc.scalar.activation(stepped[:, t, :], sums[t], COPY, scale=st_sb[:, t : t + 1])

        def weave(u):
            woven[u] = tile([P, LONG, PACK], F32, "woven%d" % u)
            nc.scalar.copy(woven[u][:], stepped[:, :, u * LONG : (u + 1) * LONG].rearrange("p t j -> p j t"))

        hid = {}

        def larger_off_vector(dst, x, y, name):
            diff = tile([P, LONG, 2], F32, name + "_diff")
            rise = tile([P, LONG, 2], F32, name + "_rise")
            nc.gpsimd.tensor_tensor(diff[:], x, y, SUB)
            nc.scalar.activation(rise[:], diff[:], RELU)
            nc.gpsimd.tensor_tensor(dst, rise[:], y, ADD)

        early_pairs = tile([P, 2, LONG, 2], F32, "early_pairs")
        first_tops = tile([P, 2, LONG, 2], F32, "first_tops")
        late_pairs = tile([P, LONG, 2, 2], F32, "late_pairs")

        def early_maxima():
            for t in range(2):
                four = early_values[t][:].rearrange("p (j q) -> p j q", q=POOL)
                larger_off_vector(early_pairs[:, t], four[:, :, 0:2], four[:, :, 2:4], "early%d" % t)
            two = early_pairs[:].rearrange("p t j e -> p j t e")
            larger_off_vector(first_tops[:, 0], two[:, :, :, 0], two[:, :, :, 1], "early_top")

        def late_round_one():
            four = late_values[:].rearrange("p t (j q) -> p j t q", q=POOL)
            nc.vector.tensor_tensor(late_pairs[:], four[:, :, :, 0:2], four[:, :, :, 2:4], MAX)

        def late_round_two():
            nc.vector.tensor_tensor(first_tops[:, 1], late_pairs[:, :, :, 0], late_pairs[:, :, :, 1], MAX)

        def first_hid():
            hid[FIRST] = tile([P, LONG, PACK], BF16, "first_hid")
            nc.gpsimd.tensor_tensor(
                hid[FIRST][:].rearrange("p j (a b) -> p j a b", b=2),
                first_tops[:].rearrange("p a j b -> p j a b"),
                woven[0][:].rearrange("p j (a b) -> p j a b", b=2),
                MULT,
            )

        pairs, tops = {}, {}

        def round_one(key, c, slots, groups):
            four = short_values[c][:].rearrange("p t (j q) -> p j t q", q=POOL)[:, slots, groups]
            nc.vector.tensor_tensor(pairs[key][:, :, groups, :], four[:, :, :, 0:2], four[:, :, :, 2:4], MAX)

        def round_two(key, width):
            tops[key] = tile([P, width, PACK], F32, "tops_" + key)
            nc.vector.tensor_tensor(tops[key][:], pairs[key][:, :, :, 0], pairs[key][:, :, :, 1], MAX)

        def make_hid(key, c, slots):
            first = CHUNKS[c][0] - LONG
            factors = woven[1][:, first + slots.start : first + slots.stop, :]
            nc.vector.tensor_tensor(hid[c][:, slots, :], tops[key][:], factors, MULT)

        products, banks, rows = {}, {}, {}

        def second_product(c):
            width = CHUNKS[c][1] - CHUNKS[c][0]
            codes = tile([P, width], U32, "codes%d" % c)
            scales = tile([P, width], U8, "scales%d" % c)
            nc.vector.quantize_mx(out=codes[:].bitcast(E4M3X4), scales=scales[:], in_=hid[c][:].rearrange("p j t -> p (j t)"))
            if c == LAST:
                for h in range(2):
                    products[c, h] = ps.tile([P, width], F32, name="product%d_%d" % (c, h))[:]
            else:
                banks[c] = ps.tile([P, 2, width], F32, name="product%d" % c)
                for h in range(2):
                    products[c, h] = banks[c][:, h, :]
            for h in range(2):
                nc.tensor.matmul_mx(
                    out=products[c, h],
                    lhsT=wb_w[:, h * P : (h + 1) * P].bitcast(E4M3X4),
                    lhsT_scale=wb_s[:, h * P : (h + 1) * P],
                    rhs=codes[:].bitcast(E4M3X4),
                    rhs_scale=scales[:],
                    start=True,
                    stop=True,
                )

        def to_sbuf(c, h, copy, in_place_of=None):
            rows[c, h] = tile([P, CHUNKS[c][1] - CHUNKS[c][0]], F32, "rows%d_%d" % (c, h), in_place_of)[:]
            copy(rows[c, h], products[c, h])

        def put(c, h):
            j0, j1 = CHUNKS[c]
            columns = out_list[:, j0 // PER_COLUMN : j1 // PER_COLUMN]
            nc.scalar.activation(pages[h][:].indirect(columns), rows[c, h], COPY, scale=so_sb[h][:])

        for t in range(PACK):
            room_for_bytes([(FIRST, t)])
        for t in range(2):
            look_up(FIRST, t)
            widen(FIRST, t)
        early_maxima()
        first_product()
        look_up(FIRST, 2)
        widen(FIRST, 2)
        apply_step(0)
        look_up(FIRST, 3)
        widen(FIRST, 3)
        for t in range(1, PACK):
            apply_step(t)
        weave(0)

        room_for_bytes([(MIDDLE, 0)], "picked0_2")
        look_up(MIDDLE, 0)
        late_round_one()
        room_for_bytes([(MIDDLE, 1)], "picked0_3")
        look_up(MIDDLE, 1)
        late_round_two()
        first_hid()
        beside_first_hid = [(MIDDLE, 2), (MIDDLE, 3), (LAST, 0), (LAST, 1)]
        room_for_bytes(beside_first_hid, "late_values")
        for c, t in beside_first_hid:
            look_up(c, t)
        for t in range(PACK):
            widen(MIDDLE, t)
        weave(1)
        for t in range(2):
            widen(LAST, t)
        second_product(FIRST)
        to_sbuf(FIRST, 0, nc.scalar.copy)
        put(FIRST, 0)

        everything = slice(0, PACK)
        whole = slice(0, SHORT)
        pairs["middle"] = tile([P, SHORT, PACK, 2], F32, "pairs_middle", "first_tops")
        round_one("middle", MIDDLE, whole, everything)
        room_for_bytes([(LAST, 2), (LAST, 3)], "woven0")
        for t in (2, 3):
            look_up(LAST, t)
            widen(LAST, t)
        round_two("middle", SHORT)
        to_sbuf(FIRST, 1, nc.scalar.copy, "ca3")
        put(FIRST, 1)

        pieces = [("piece%d" % i, slice(i * PIECE, (i + 1) * PIECE)) for i in range(2)]
        for key, slots in pieces:
            pairs[key] = tile([P, PIECE, PACK, 2], F32, "pairs_" + key)
            round_one(key, LAST, slots, slice(0, 2))
        hid[MIDDLE] = tile([P, SHORT, PACK], BF16, "middle_hid")
        make_hid("middle", MIDDLE, whole)
        for key, slots in pieces:
            round_one(key, LAST, slots, slice(2, PACK))
        second_product(MIDDLE)
        for key, slots in pieces:
            round_two(key, PIECE)
        middle_rows = tile([P, 2, SHORT], F32, "middle_rows")
        nc.vector.tensor_copy(middle_rows[:], banks[MIDDLE][:])
        for h in range(2):
            rows[MIDDLE, h] = middle_rows[:, h, :]
            put(MIDDLE, h)
        hid[LAST] = tile([P, SHORT, PACK], BF16, "last_hid")
        for key, slots in pieces:
            make_hid(key, LAST, slots)
        second_product(LAST)
        for h in range(2):
            to_sbuf(LAST, h, nc.vector.tensor_copy)
        for h in range(2):
            put(LAST, h)

        nc.sync.dma_start(out[0:P, :], pages[0][:])
        nc.scalar.dma_start(out[P : 2 * P, :], pages[1][:])
